import numpy as np
import ml_dtypes


def mxq(x, axis, fmt="e4m3"):
    dtype, down = {"e4m3": (ml_dtypes.float8_e4m3fn, 7), "e5m2": (ml_dtypes.float8_e5m2, 14)}[fmt]
    v = np.moveaxis(np.asarray(x, np.float32).astype(ml_dtypes.bfloat16).astype(np.float64), axis, -1)
    blocks = v.reshape(v.shape[:-1] + (-1, 32))
    amax = np.abs(blocks).max(-1, keepdims=True)
    byte = np.maximum(np.where(amax > 0, np.frexp(amax)[1] - 1 + 127, 0) - down, 1)
    scale = np.exp2(byte - 127.0)
    codes = (blocks / scale).astype(np.float32).astype(dtype).astype(np.float64)
    return np.moveaxis((codes * scale).reshape(v.shape), -1, axis)


WIDE = False


def mx_kscale(k):
    if not WIDE:
        return np.ones(k)
    levels = np.array([10, -10, 5, -5, 0])
    if k % 512:
        return np.exp2(np.random.permutation(np.resize(levels, k // 32))).repeat(32)
    a = np.empty((k // 512, 16))
    for p in range(k // 512):
        a[p, :8] = np.random.permutation(np.resize(levels, 8))
        for g in range(8):
            far = levels[np.abs(levels - a[p, g]) >= 10]
            a[p, g + 8] = far[np.random.randint(len(far))]
    return np.exp2(a.ravel()).repeat(32)


def f64(x):
    return np.asarray(x).astype(np.float64)


def striped(idx):
    return np.tile(idx.reshape(-1, 16).T, (8, 1)).astype(np.uint16)


def unstriped(offs):
    return offs[:16].T.reshape(-1).astype(np.int64)


def striped8(idx):
    return np.concatenate([x.reshape(-1, 16).T for x in idx]).astype(np.uint16)


def runs(offs, k):
    lists = np.stack([offs[16 * r : 16 * r + 16].T.reshape(-1) for r in range(8)]).astype(np.int64)
    return lists[np.arange(k) % 512 // 64]


def pack_weight(w):
    k, n = w.shape
    w = f64(np.asarray(w, np.float32).astype(ml_dtypes.bfloat16)).reshape(k // 32, 32, n)
    amax = np.abs(w).max(1)
    byte = np.clip(np.where(amax > 0, np.frexp(amax)[1] - 1 + 127 - 7, 1), 1, 254)
    scaled = (w * np.exp2(127.0 - byte)[:, None, :]).reshape(k, n).astype(np.float32)
    words = np.ascontiguousarray(scaled.reshape(k // 512, 128, 4, n).transpose(0, 1, 3, 2)).astype(ml_dtypes.float8_e4m3fn).view(np.uint8)
    return words, np.ascontiguousarray(byte.astype(np.uint8).reshape(k // 512, 16, n))


def unpack_weight(words, scales):
    g, p, n, _ = words.shape
    vals = np.ascontiguousarray(words).view(ml_dtypes.float8_e4m3fn).astype(np.float64) * np.repeat(np.exp2(scales.astype(np.float64) - 127.0), 8, axis=1)[..., None]
    return vals.transpose(0, 1, 3, 2).reshape(g * 512, n)


def sigmoid(v):
    return 1.0 / (1.0 + np.exp(-np.maximum(v, -700.0)))


K, T, S, N, H = 512, 2048, 512, 512, 512


def setup_inputs():
    n = np.random.standard_normal
    s = mx_kscale(K)[:, None]
    u = mx_kscale(H)
    packed_xT = pack_weight(n((K, T)) * s)
    return {
        "x_words": packed_xT[0],
        "x_scales": packed_xT[1],
        "w1": (n((K, H)) / np.sqrt(K) / s).astype(np.float32),
        "gn": (np.random.uniform(0.5, 1.5, (H, 1)) * u[:, None]).astype(np.float32),
        "w2": (n((H, N)) / np.sqrt(H) / u[:, None]).astype(np.float32),
        "gm": (np.random.uniform(0.5, 1.5, (H, 1)) * u[:, None]).astype(np.float32),
        "w3": (n((H, N)) / np.sqrt(H) / u[:, None]).astype(np.float32),
        "offs": striped(np.random.permutation(T)[:S]),
        "n1": striped8(np.stack([np.random.permutation(S) for _ in range(8)])),
        "n2": striped8(np.stack([np.random.permutation(S) for _ in range(8)])),
        "n3": striped8(np.stack([np.random.permutation(S) for _ in range(8)])),
        "n4": striped8(np.stack([np.random.permutation(S) for _ in range(8)])),
        "n5": striped8(np.stack([np.random.permutation(S) for _ in range(8)])),
        "n6": striped8(np.stack([np.random.permutation(S) for _ in range(8)])),
    }


def reference(x_words, x_scales, w1, gn, w2, gm, w3, offs, n1, n2, n3, n4, n5, n6):
    xq = unpack_weight(x_words, x_scales)[:, unstriped(offs)]
    y = mxq(f64(w1), 0, "e4m3").T @ xq
    z = f64(gn) * ((y[np.arange(H)[:, None], runs(n1, H)]) / (np.abs(y) + np.abs(y[np.arange(H)[:, None], runs(n2, H)]) + 0.5))
    a = mxq(f64(w2), 0, "e4m3").T @ mxq(z, 0, "e4m3")
    z2 = f64(gm) * (np.maximum(y * (sigmoid(y[np.arange(H)[:, None], runs(n3, H)])), y[np.arange(H)[:, None], runs(n4, H)]))
    b = mxq(f64(w3), 0, "e4m3").T @ mxq(z2, 0, "e4m3")
    return (a - (a[np.arange(N)[:, None], runs(n5, N)])) / (np.abs(b) + np.abs(b[np.arange(N)[:, None], runs(n6, N)]) + 0.5)

@@ -1,0 +1,177 @@
+from contextlib import ExitStack
+
+import concourse.mybir as mybir
+
+K, T, S, N, H = 512, 2048, 512, 512, 512
+FLOPS = 3 * 2 * 512 * 512 * 512
+
+F32 = mybir.dt.float32
+BF16 = mybir.dt.bfloat16
+I32 = mybir.dt.int32
+U32 = mybir.dt.uint32
+U16 = mybir.dt.uint16
+U8 = mybir.dt.uint8
+FP8X4 = mybir.dt.float8_e4m3fn_x4
+ALU = mybir.AluOpType
+ACT = mybir.ActivationFunctionType
+
+P = 128
+PACK = 4
+WIN = 2 * S
+
+
+def tile_picked_forknormbnorm2gmax_none_p_kernel(
+    tc, x_words, x_scales, w1, gn, w2, gm, w3, offs, n1, n2, n3, n4, n5, n6, out
+):
+    nc = tc.nc
+    with ExitStack() as ctx:
+        keep = ctx.enter_context(tc.tile_pool(name="keep", bufs=1))
+        psum = ctx.enter_context(tc.psum_pool(name="psum", bufs=1))
+
+        def f32_tiles(name, width):
+            return [keep.tile([P, width], F32, name="%s%d" % (name, t)) for t in range(PACK)]
+
+        def load_list(name, src):
+            tile = keep.tile([P, S // 16], U16, name=name)
+            nc.sync.dma_start(tile[:], src)
+            return tile
+
+        warm = keep.tile([P, 1], F32, name="warm")
+        warm_out = keep.tile([P, 1], F32, name="warm_out")
+        xs = keep.tile([P, T], U8, name="xs")
+        nc.vector.memset(xs[:].bitcast(I32), 0)
+        nc.vector.memset(warm[:], 0.0)
+        for q in range(4):
+            nc.scalar.dma_start(xs[32 * q : 32 * q + 4, :].bitcast(I32), x_scales[0, 4 * q : 4 * q + 4, :].bitcast(I32))
+        nc.scalar.activation(warm_out[:], warm[:], ACT.Sigmoid)
+
+        l0 = load_list("l0", offs)
+        xw = keep.tile([P, T], U32, name="xw")
+        nc.sync.dma_start(xw[:].bitcast(I32), x_words[0].rearrange("p n t -> p (n t)").bitcast(I32))
+        w1_raw = [keep.tile([P, PACK, H // 2], F32, name="w1_raw%d" % h) for h in range(2)]
+        for h in range(2):
+            nc.sync.dma_start(w1_raw[h][:], w1.rearrange("(p j) c -> p j c", j=PACK)[:, :, h * 256 : (h + 1) * 256])
+        l2 = load_list("l2", n2)
+        l4 = load_list("l4", n4)
+        l3 = load_list("l3", n3)
+        gm_sb = keep.tile([P, PACK], F32, name="gm_sb")
+        nc.sync.dma_start(gm_sb[:], gm.rearrange("(p t) o -> p (t o)", t=PACK))
+        gn_sb = keep.tile([P, PACK], F32, name="gn_sb")
+        nc.sync.dma_start(gn_sb[:], gn.rearrange("(p t) o -> p (t o)", t=PACK))
+        w3_raw = keep.tile([P, PACK, N], F32, name="w3_raw")
+        nc.sync.dma_start(w3_raw[:], w3.rearrange("(p j) c -> p j c", j=PACK))
+        w2_raw = keep.tile([P, PACK, N], F32, name="w2_raw")
+        nc.sync.dma_start(w2_raw[:], w2.rearrange("(p j) c -> p j c", j=PACK))
+        l1 = load_list("l1", n1)
+        l6 = load_list("l6", n6)
+        l5 = load_list("l5", n5)
+
+        win_y = f32_tiles("win_y", WIN)
+        win_abs = f32_tiles("win_abs", WIN)
+        win_g = f32_tiles("win_g", WIN)
+        for t in range(PACK):
+            nc.vector.memset(win_abs[t][:, S:], 0.0)
+        for t in range(PACK):
+            nc.vector.memset(win_g[t][:, S:], 0.0)
+
+        xq_s = keep.tile([P, S], U8, name="xq_s", align_bytes=64)
+        nc.vector.tensor_copy(xq_s[:], xs[:].indirect(l0[:]))
+        xq_w = keep.tile([P, S], U32, name="xq_w", align_bytes=64)
+        nc.vector.tensor_copy(xq_w[:], xw[:].indirect(l0[:]))
+
+        def dealt(wb, m0, m1):
+            return wb[:].rearrange("p (t m j) -> p m j t", t=PACK, j=PACK)[:, m0:m1, :, :]
+
+        def raw_view(raw):
+            return raw[:].rearrange("p j (m t) -> p m j t", t=PACK)
+
+        def mx_tiles(name):
+            wb = keep.tile([P, PACK * 512], BF16, name=name + "_bf", align_bytes=64)
+            codes = keep.tile([P, 512], U32, name=name + "_codes", align_bytes=64)
+            scales = keep.tile([P, 512], U8, name=name + "_scales", align_bytes=64)
+            return wb, codes, scales
+
+        def quantize(tiles, c0, c1):
+            wb, codes, scales = tiles
+            nc.vector.quantize_mx(out=codes[:, c0:c1].bitcast(FP8X4), scales=scales[:, c0:c1], in_=wb[:, PACK * c0 : PACK * c1])
+
+        def product(bank, w_tiles, t, codes, scales):
+            cols = slice(t * P, (t + 1) * P)
+            nc.tensor.matmul_mx(
+                out=bank[:], lhsT=w_tiles[1][:, cols].bitcast(FP8X4), lhsT_scale=w_tiles[2][:, cols],
+                rhs=codes[:].bitcast(FP8X4), rhs_scale=scales[:], start=True, stop=True,
+            )
+
+        w1q, w2q, w3q, zq, z2q = (mx_tiles(n) for n in ("w1", "w2", "w3", "z", "z2"))
+        for h in range(2):
+            nc.vector.tensor_copy(dealt(w1q[0], 64 * h, 64 * (h + 1)), raw_view(w1_raw[h]))
+        banks = [psum.tile([P, S], F32, name="bank%d" % b) for b in range(8)]
+        quantize(w1q, 0, 128)
+        quantize(w1q, 128, 256)
+        quantize(w1q, 256, 512)
+        for t in range(PACK):
+            product(banks[t], w1q, t, xq_w, xq_s)
+
+        den = f32_tiles("den", S)
+        sig = f32_tiles("sig", S)
+        other = f32_tiles("other", S)
+        gated = f32_tiles("gated", S)
+        larger = keep.tile([P, PACK, S], F32, name="larger")
+        root = keep.tile([P, PACK, S], F32, name="root")
+        half_z = keep.tile([P, PACK, S], F32, name="half_z")
+
+        def woven_out(tiles):
+            return tiles[0][:].rearrange("p (c i t) -> p c t i", i=4, t=PACK)
+
+        def woven_in(planes):
+            return planes[:].rearrange("p t (c i) -> p c t i", i=4)
+
+        for t in range(PACK):
+            nc.scalar.activation(win_y[t][:, :S], banks[t][:], ACT.Copy)
+            nc.scalar.activation(win_y[t][:, S:], banks[t][:], ACT.Abs)
+            nc.scalar.activation(win_abs[t][:, :S], banks[t][:], ACT.Abs)
+            nc.vector.tensor_copy(other[t][:], win_y[t][:].indirect(l4[:]))
+            nc.vector.tensor_tensor(den[t][:], win_abs[t][:].indirect(l2[:]), win_y[t][:, S:], ALU.add)
+        for t in range(PACK):
+            nc.scalar.activation(sig[t][:], win_y[t][:].indirect(l3[:]), ACT.Sigmoid)
+            nc.vector.tensor_tensor(gated[t][:], win_y[t][:, :S], sig[t][:], ALU.mult)
+        for t in range(PACK):
+            nc.vector.tensor_tensor(larger[:, t, :], gated[t][:], other[t][:], ALU.max)
+        nc.scalar.copy(dealt(w3q[0], 0, 128), raw_view(w3_raw))
+        gm_wide = gm_sb[:].unsqueeze(1).unsqueeze(3).to_broadcast([P, S // 4, PACK, 4])
+        nc.vector.tensor_tensor(woven_out(z2q), woven_in(larger), gm_wide, ALU.mult)
+        quantize(w3q, 0, 512)
+        quantize(z2q, 0, 512)
+        for t in range(PACK):
+            product(banks[4 + t], w3q, t, z2q[1], z2q[2])
+        for t in range(PACK):
+            nc.scalar.activation(root[:, t, :], den[t][:], ACT.Abs_reciprocal_sqrt, bias=0.5)
+            nc.scalar.activation(win_g[t][:, :S], banks[t][:], ACT.Copy, scale=gn_sb[:, t : t + 1])
+            nc.vector.tensor_tensor(half_z[:, t, :], win_g[t][:].indirect(l1[:]), root[:, t, :], ALU.mult)
+        nc.scalar.copy(dealt(w2q[0], 0, 128), raw_view(w2_raw))
+        nc.vector.tensor_tensor(woven_out(zq), woven_in(half_z), woven_in(root), ALU.mult)
+        quantize(w2q, 0, 512)
+        quantize(zq, 0, 512)
+        for t in range(PACK):
+            product(banks[t], w2q, t, zq[1], zq[2])
+
+        b_abs = f32_tiles("b_abs", S)
+        a_own = f32_tiles("a_own", S)
+        den_b = f32_tiles("den_b", S)
+        root_b = f32_tiles("root_b", S)
+        inv_b = f32_tiles("inv_b", S)
+        diff = f32_tiles("diff", S)
+        res = f32_tiles("res", S)
+        for t in range(PACK):
+            nc.scalar.activation(win_abs[t][:, :S], banks[4 + t][:], ACT.Abs)
+            nc.scalar.activation(b_abs[t][:], banks[4 + t][:], ACT.Abs)
+            nc.vector.tensor_tensor(den_b[t][:], win_abs[t][:].indirect(l6[:]), b_abs[t][:], ALU.add)
+        out_rows = out.rearrange("(p t) n -> p t n", t=PACK)
+        for t in range(PACK):
+            nc.scalar.activation(win_g[t][:, :S], banks[t][:], ACT.Copy)
+            nc.scalar.activation(a_own[t][:], banks[t][:], ACT.Copy)
+            nc.scalar.activation(root_b[t][:], den_b[t][:], ACT.Abs_reciprocal_sqrt, bias=0.5)
+            nc.scalar.activation(inv_b[t][:], root_b[t][:], ACT.Square)
+            nc.vector.tensor_tensor(diff[t][:], win_g[t][:].indirect(l5[:]), a_own[t][:], ALU.subtract)
+            nc.vector.scalar_tensor_tensor(res[t][:], diff[t][:], -1.0, inv_b[t][:], ALU.mult, ALU.mult)
+            nc.sync.dma_start(out_rows[:, t, :], res[t][:])

@@ -41,28 +41,29 @@ def tile_picked_forknormbnorm2gmax_none_p_kernel(
         xs = keep.tile([P, T], U8, name="xs")
         nc.vector.memset(xs[:].bitcast(I32), 0)
         nc.vector.memset(warm[:], 0.0)
-        for q in range(4):
-            nc.scalar.dma_start(xs[32 * q : 32 * q + 4, :].bitcast(I32), x_scales[0, 4 * q : 4 * q + 4, :].bitcast(I32))
         nc.scalar.activation(warm_out[:], warm[:], ACT.Sigmoid)
 
         l0 = load_list("l0", offs)
+        w1_raw = [keep.tile([P, PACK, H // 2], F32, name="w1_raw%d" % h) for h in range(2)]
+        w1_rows = w1.rearrange("(p j) c -> p j c", j=PACK)
+        nc.sync.dma_start(w1_raw[0][:], w1_rows[:, :, :256])
+        for q in range(4):
+            nc.sync.dma_start(xs[32 * q : 32 * q + 4, :].bitcast(I32), x_scales[0, 4 * q : 4 * q + 4, :].bitcast(I32))
         xw = keep.tile([P, T], U32, name="xw")
         nc.sync.dma_start(xw[:].bitcast(I32), x_words[0].rearrange("p n t -> p (n t)").bitcast(I32))
-        w1_raw = [keep.tile([P, PACK, H // 2], F32, name="w1_raw%d" % h) for h in range(2)]
-        for h in range(2):
-            nc.sync.dma_start(w1_raw[h][:], w1.rearrange("(p j) c -> p j c", j=PACK)[:, :, h * 256 : (h + 1) * 256])
-        l2 = load_list("l2", n2)
+        nc.sync.dma_start(w1_raw[1][:], w1_rows[:, :, 256:])
         l4 = load_list("l4", n4)
         l3 = load_list("l3", n3)
+        l2 = load_list("l2", n2)
         gm_sb = keep.tile([P, PACK], F32, name="gm_sb")
         nc.sync.dma_start(gm_sb[:], gm.rearrange("(p t) o -> p (t o)", t=PACK))
-        gn_sb = keep.tile([P, PACK], F32, name="gn_sb")
-        nc.sync.dma_start(gn_sb[:], gn.rearrange("(p t) o -> p (t o)", t=PACK))
         w3_raw = keep.tile([P, PACK, N], F32, name="w3_raw")
         nc.sync.dma_start(w3_raw[:], w3.rearrange("(p j) c -> p j c", j=PACK))
+        gn_sb = keep.tile([P, PACK], F32, name="gn_sb")
+        nc.sync.dma_start(gn_sb[:], gn.rearrange("(p t) o -> p (t o)", t=PACK))
+        l1 = load_list("l1", n1)
         w2_raw = keep.tile([P, PACK, N], F32, name="w2_raw")
         nc.sync.dma_start(w2_raw[:], w2.rearrange("(p j) c -> p j c", j=PACK))
-        l1 = load_list("l1", n1)
         l6 = load_list("l6", n6)
         l5 = load_list("l5", n5)
 
@@ -70,9 +71,9 @@ def tile_picked_forknormbnorm2gmax_none_p_kernel(
         win_abs = f32_tiles("win_abs", WIN)
         win_g = f32_tiles("win_g", WIN)
         for t in range(PACK):
-            nc.vector.memset(win_abs[t][:, S:], 0.0)
-        for t in range(PACK):
-            nc.vector.memset(win_g[t][:, S:], 0.0)
+            nc.vector.memset(win_y[t][:, S:], 0.0)
+            nc.gpsimd.memset(win_abs[t][:, S:], 0.0)
+            nc.scalar.activation(win_g[t][:, S:], warm[:].to_broadcast([P, S]), ACT.Copy)
 
         xq_s = keep.tile([P, S], U8, name="xq_s", align_bytes=64)
         nc.vector.tensor_copy(xq_s[:], xs[:].indirect(l0[:]))
@@ -112,13 +113,18 @@ def tile_picked_forknormbnorm2gmax_none_p_kernel(
         for t in range(PACK):
             product(banks[t], w1q, t, xq_w, xq_s)
 
+        own_abs = f32_tiles("own_abs", S)
         den = f32_tiles("den", S)
         sig = f32_tiles("sig", S)
         other = f32_tiles("other", S)
         gated = f32_tiles("gated", S)
+        root = f32_tiles("root", S)
+        inv = f32_tiles("inv", S)
         larger = keep.tile([P, PACK, S], F32, name="larger")
-        root = keep.tile([P, PACK, S], F32, name="root")
-        half_z = keep.tile([P, PACK, S], F32, name="half_z")
+        z_planes = keep.tile([P, PACK, S], F32, name="z_planes")
+
+        root_z = keep.tile([P, PACK, S], F32, name="root_z")
+        z2_planes = keep.tile([P, PACK, S // 2], BF16, name="z2_planes")
 
         def woven_out(tiles):
             return tiles[0][:].rearrange("p (c i t) -> p c t i", i=4, t=PACK)
@@ -128,50 +134,87 @@ def tile_picked_forknormbnorm2gmax_none_p_kernel(
 
         for t in range(PACK):
             nc.scalar.activation(win_y[t][:, :S], banks[t][:], ACT.Copy)
-            nc.scalar.activation(win_y[t][:, S:], banks[t][:], ACT.Abs)
-            nc.scalar.activation(win_abs[t][:, :S], banks[t][:], ACT.Abs)
             nc.vector.tensor_copy(other[t][:], win_y[t][:].indirect(l4[:]))
-            nc.vector.tensor_tensor(den[t][:], win_abs[t][:].indirect(l2[:]), win_y[t][:, S:], ALU.add)
         for t in range(PACK):
             nc.scalar.activation(sig[t][:], win_y[t][:].indirect(l3[:]), ACT.Sigmoid)
             nc.vector.tensor_tensor(gated[t][:], win_y[t][:, :S], sig[t][:], ALU.mult)
+            if t > 0:
+                nc.vector.tensor_tensor(larger[:, t - 1, :], gated[t - 1][:], other[t - 1][:], ALU.max)
+        nc.vector.tensor_tensor(larger[:, PACK - 1, :], gated[PACK - 1][:], other[PACK - 1][:], ALU.max)
         for t in range(PACK):
-            nc.vector.tensor_tensor(larger[:, t, :], gated[t][:], other[t][:], ALU.max)
+            nc.scalar.activation(win_abs[t][:, :S], banks[t][:], ACT.Abs)
+            nc.sync.dma_start(own_abs[t][:], win_abs[t][:, :S])
+
+        def size_sum(total, t, offsets):
+            nc.vector.tensor_tensor(total, win_abs[t][:].indirect(offsets[:]), own_abs[t][:], ALU.add)
+
         nc.scalar.copy(dealt(w3q[0], 0, 128), raw_view(w3_raw))
-        gm_wide = gm_sb[:].unsqueeze(1).unsqueeze(3).to_broadcast([P, S // 4, PACK, 4])
-        nc.vector.tensor_tensor(woven_out(z2q), woven_in(larger), gm_wide, ALU.mult)
+        for t in range(PACK):
+            nc.scalar.activation(z2_planes[:, t, :], larger[:, t, S // 2 :], ACT.Copy, scale=gm_sb[:, t : t + 1])
+        nc.scalar.copy(woven_out(z2q)[:, S // 8 :], woven_in(z2_planes))
+        size_sum(den[0][:], 0, l2)
+        gm_wide = gm_sb[:].unsqueeze(1).unsqueeze(3).to_broadcast([P, S // 8, PACK, 4])
+        nc.vector.tensor_tensor(woven_out(z2q)[:, : S // 8], woven_in(larger)[:, : S // 8], gm_wide, ALU.mult)
+        size_sum(den[1][:], 1, l2)
         quantize(w3q, 0, 512)
         quantize(z2q, 0, 512)
         for t in range(PACK):
             product(banks[4 + t], w3q, t, z2q[1], z2q[2])
-        for t in range(PACK):
-            nc.scalar.activation(root[:, t, :], den[t][:], ACT.Abs_reciprocal_sqrt, bias=0.5)
-            nc.scalar.activation(win_g[t][:, :S], banks[t][:], ACT.Copy, scale=gn_sb[:, t : t + 1])
-            nc.vector.tensor_tensor(half_z[:, t, :], win_g[t][:].indirect(l1[:]), root[:, t, :], ALU.mult)
-        nc.scalar.copy(dealt(w2q[0], 0, 128), raw_view(w2_raw))
-        nc.vector.tensor_tensor(woven_out(zq), woven_in(half_z), woven_in(root), ALU.mult)
-        quantize(w2q, 0, 512)
-        quantize(zq, 0, 512)
-        for t in range(PACK):
-            product(banks[t], w2q, t, zq[1], zq[2])
+        for t in range(2, PACK):
+            size_sum(den[t][:], t, l2)
 
-        b_abs = f32_tiles("b_abs", S)
-        a_own = f32_tiles("a_own", S)
-        den_b = f32_tiles("den_b", S)
-        root_b = f32_tiles("root_b", S)
-        inv_b = f32_tiles("inv_b", S)
-        diff = f32_tiles("diff", S)
-        res = f32_tiles("res", S)
+        root_b, inv_b, a_own = sig, other, gated
+        for t in range(PACK):
+            nc.scalar.activation(root_z[:, t, :], den[t][:], ACT.Abs_reciprocal_sqrt, bias=0.5)
+            nc.scalar.activation(win_g[t][:, :S], banks[t][:], ACT.Copy, scale=gn_sb[:, t : t + 1])
+            nc.vector.tensor_tensor(z_planes[:, t, :], win_g[t][:].indirect(l1[:]), root_z[:, t, :], ALU.mult)
         for t in range(PACK):
             nc.scalar.activation(win_abs[t][:, :S], banks[4 + t][:], ACT.Abs)
-            nc.scalar.activation(b_abs[t][:], banks[4 + t][:], ACT.Abs)
-            nc.vector.tensor_tensor(den_b[t][:], win_abs[t][:].indirect(l6[:]), b_abs[t][:], ALU.add)
-        out_rows = out.rearrange("(p t) n -> p t n", t=PACK)
+            nc.sync.dma_start(own_abs[t][:], win_abs[t][:, :S])
+        nc.scalar.copy(dealt(w2q[0], 0, 128), raw_view(w2_raw))
+        nc.vector.tensor_tensor(woven_out(zq), woven_in(z_planes), woven_in(root_z), ALU.mult)
+        den_b = [den[0][:], den[1][:], den[2][:], den[3][:]]
+        size_sum(den_b[0], 0, l6)
+        quantize(zq, 0, 512)
+        quantize(w2q, 0, 512)
         for t in range(PACK):
-            nc.scalar.activation(win_g[t][:, :S], banks[t][:], ACT.Copy)
-            nc.scalar.activation(a_own[t][:], banks[t][:], ACT.Copy)
-            nc.scalar.activation(root_b[t][:], den_b[t][:], ACT.Abs_reciprocal_sqrt, bias=0.5)
+            product(banks[t], w2q, t, zq[1], zq[2])
+        for t in range(1, PACK):
+            size_sum(den_b[t], t, l6)
+
+        diff, res = root, inv
+        out_rows = out.rearrange("(p t) n -> p t n", t=PACK)
+
+        def inverse_b(t):
+            nc.scalar.activation(root_b[t][:], den_b[t], ACT.Abs_reciprocal_sqrt, bias=0.5)
             nc.scalar.activation(inv_b[t][:], root_b[t][:], ACT.Square)
-            nc.vector.tensor_tensor(diff[t][:], win_g[t][:].indirect(l5[:]), a_own[t][:], ALU.subtract)
-            nc.vector.scalar_tensor_tensor(res[t][:], diff[t][:], -1.0, inv_b[t][:], ALU.mult, ALU.mult)
-            nc.sync.dma_start(out_rows[:, t, :], res[t][:])
+
+        def difference(t, cols):
+            offsets = l5[:, cols.start // 16 : cols.stop // 16]
+            nc.vector.tensor_tensor(diff[t][:, cols], win_y[t][:].indirect(offsets), a_own[t][:, cols], ALU.subtract)
+
+        def join(t, cols):
+            nc.vector.scalar_tensor_tensor(res[t][:, cols], diff[t][:, cols], -1.0, inv_b[t][:, cols], ALU.mult, ALU.mult)
+            nc.sync.dma_start(out_rows[:, t, cols], res[t][:, cols])
+
+        whole = slice(0, S)
+        halves = (slice(0, S // 2), slice(S // 2, S))
+        inverse_b(0)
+        for t in range(PACK):
+            nc.scalar.activation(win_y[t][:, :S], banks[t][:], ACT.Copy)
+            if t < 1:
+                nc.scalar.activation(a_own[t][:], banks[t][:], ACT.Copy)
+            else:
+                nc.sync.dma_start(a_own[t][:], win_y[t][:, :S])
+        for t in range(1, PACK):
+            inverse_b(t)
+        difference(0, whole)
+        difference(1, whole)
+        join(0, whole)
+        join(1, whole)
+        difference(2, whole)
+        difference(3, halves[0])
+        join(2, whole)
+        difference(3, halves[1])
+        for cols in halves:
+            join(3, cols)

@@ -1,6 +1,7 @@
 from contextlib import ExitStack
 
 import concourse.mybir as mybir
+from concourse.masks import make_identity
 
 K, T, S, N, H = 512, 2048, 512, 512, 512
 FLOPS = 3 * 2 * 512 * 512 * 512
@@ -39,7 +40,7 @@ def tile_picked_forknormbnorm2gmax_none_p_kernel(
         warm = keep.tile([P, 1], F32, name="warm")
         warm_out = keep.tile([P, 1], F32, name="warm_out")
         xs = keep.tile([P, T], U8, name="xs")
-        nc.vector.memset(xs[:].bitcast(I32), 0)
+        nc.gpsimd.memset(xs[:].bitcast(I32), 0)
         nc.vector.memset(warm[:], 0.0)
         nc.scalar.activation(warm_out[:], warm[:], ACT.Sigmoid)
 
@@ -72,7 +73,7 @@ def tile_picked_forknormbnorm2gmax_none_p_kernel(
         win_g = f32_tiles("win_g", WIN)
         for t in range(PACK):
             nc.vector.memset(win_y[t][:, S:], 0.0)
-            nc.gpsimd.memset(win_abs[t][:, S:], 0.0)
+            nc.scalar.activation(win_abs[t][:, S:], warm[:].to_broadcast([P, S]), ACT.Copy)
             nc.scalar.activation(win_g[t][:, S:], warm[:].to_broadcast([P, S]), ACT.Copy)
 
         xq_s = keep.tile([P, S], U8, name="xq_s", align_bytes=64)
@@ -106,34 +107,52 @@ def tile_picked_forknormbnorm2gmax_none_p_kernel(
         w1q, w2q, w3q, zq, z2q = (mx_tiles(n) for n in ("w1", "w2", "w3", "z", "z2"))
         for h in range(2):
             nc.vector.tensor_copy(dealt(w1q[0], 64 * h, 64 * (h + 1)), raw_view(w1_raw[h]))
-        banks = [psum.tile([P, S], F32, name="bank%d" % b) for b in range(8)]
+        def banks(name, tag):
+            return [psum.tile([P, S], F32, name="%s%d" % (name, t), tag="%s%d" % (tag, t)) for t in range(PACK)]
+
+        ident = keep.tile([P, P], F32, name="ident")
+        make_identity(nc, ident[:])
+        y_ps = banks("y_ps", "product")
         quantize(w1q, 0, 128)
         quantize(w1q, 128, 256)
         quantize(w1q, 256, 512)
         for t in range(PACK):
-            product(banks[t], w1q, t, xq_w, xq_s)
+            product(y_ps[t], w1q, t, xq_w, xq_s)
 
-        own_abs = f32_tiles("own_abs", S)
-        den = f32_tiles("den", S)
+        far_abs = f32_tiles("far_abs", S)
         sig = f32_tiles("sig", S)
         other = f32_tiles("other", S)
         gated = f32_tiles("gated", S)
         root = f32_tiles("root", S)
         inv = f32_tiles("inv", S)
         larger = keep.tile([P, PACK, S], F32, name="larger")
-        z_planes = keep.tile([P, PACK, S], F32, name="z_planes")
-
-        root_z = keep.tile([P, PACK, S], F32, name="root_z")
+        picked = keep.tile([P, PACK, S], F32, name="picked")
         z2_planes = keep.tile([P, PACK, S // 2], BF16, name="z2_planes")
 
         def woven_out(tiles):
             return tiles[0][:].rearrange("p (c i t) -> p c t i", i=4, t=PACK)
 
         def woven_in(planes):
-            return planes[:].rearrange("p t (c i) -> p c t i", i=4)
+            return planes.rearrange("p t (c i) -> p c t i", i=4)
+
+        def block(b):
+            return slice(b * P, (b + 1) * P)
+
+        def turned_sum(bank, first, second):
+            for b in range(S // P):
+                nc.tensor.matmul(bank[:, block(b)], lhsT=first[:, block(b)], rhs=ident[:], is_transpose=True, start=True, stop=False)
+                nc.tensor.matmul(bank[:, block(b)], lhsT=second[:, block(b)], rhs=ident[:], is_transpose=True, start=False, stop=True)
+
+        def size_sum(bank, t, offsets):
+            nc.vector.tensor_copy(far_abs[t][:], win_abs[t][:].indirect(offsets[:]))
+            turned_sum(bank, win_abs[t], far_abs[t])
+
+        def inverse(t, bank):
+            nc.scalar.activation(root[t][:], bank[:], ACT.Abs_reciprocal_sqrt, bias=0.5)
+            nc.scalar.activation(inv[t][:], root[t][:], ACT.Square)
 
         for t in range(PACK):
-            nc.scalar.activation(win_y[t][:, :S], banks[t][:], ACT.Copy)
+            nc.scalar.activation(win_y[t][:, :S], y_ps[t][:], ACT.Copy)
             nc.vector.tensor_copy(other[t][:], win_y[t][:].indirect(l4[:]))
         for t in range(PACK):
             nc.scalar.activation(sig[t][:], win_y[t][:].indirect(l3[:]), ACT.Sigmoid)
@@ -142,77 +161,82 @@ def tile_picked_forknormbnorm2gmax_none_p_kernel(
                 nc.vector.tensor_tensor(larger[:, t - 1, :], gated[t - 1][:], other[t - 1][:], ALU.max)
         nc.vector.tensor_tensor(larger[:, PACK - 1, :], gated[PACK - 1][:], other[PACK - 1][:], ALU.max)
         for t in range(PACK):
-            nc.scalar.activation(win_abs[t][:, :S], banks[t][:], ACT.Abs)
-            nc.sync.dma_start(own_abs[t][:], win_abs[t][:, :S])
-
-        def size_sum(total, t, offsets):
-            nc.vector.tensor_tensor(total, win_abs[t][:].indirect(offsets[:]), own_abs[t][:], ALU.add)
-
-        nc.scalar.copy(dealt(w3q[0], 0, 128), raw_view(w3_raw))
+            nc.scalar.activation(win_abs[t][:, :S], y_ps[t][:], ACT.Abs)
         for t in range(PACK):
             nc.scalar.activation(z2_planes[:, t, :], larger[:, t, S // 2 :], ACT.Copy, scale=gm_sb[:, t : t + 1])
-        nc.scalar.copy(woven_out(z2q)[:, S // 8 :], woven_in(z2_planes))
-        size_sum(den[0][:], 0, l2)
+        nc.scalar.copy(woven_out(z2q)[:, S // 8 :], woven_in(z2_planes[:]))
+        den_ps = banks("den_ps", "turned")
+        size_sum(den_ps[0], 0, l2)
         gm_wide = gm_sb[:].unsqueeze(1).unsqueeze(3).to_broadcast([P, S // 8, PACK, 4])
-        nc.vector.tensor_tensor(woven_out(z2q)[:, : S // 8], woven_in(larger)[:, : S // 8], gm_wide, ALU.mult)
-        size_sum(den[1][:], 1, l2)
-        quantize(w3q, 0, 512)
+        nc.vector.tensor_tensor(woven_out(z2q)[:, : S // 8], woven_in(larger[:])[:, : S // 8], gm_wide, ALU.mult)
+        for t in range(1, PACK):
+            size_sum(den_ps[t], t, l2)
         quantize(z2q, 0, 512)
-        for t in range(PACK):
-            product(banks[4 + t], w3q, t, z2q[1], z2q[2])
-        for t in range(2, PACK):
-            size_sum(den[t][:], t, l2)
 
-        root_b, inv_b, a_own = sig, other, gated
-        for t in range(PACK):
-            nc.scalar.activation(root_z[:, t, :], den[t][:], ACT.Abs_reciprocal_sqrt, bias=0.5)
-            nc.scalar.activation(win_g[t][:, :S], banks[t][:], ACT.Copy, scale=gn_sb[:, t : t + 1])
-            nc.vector.tensor_tensor(z_planes[:, t, :], win_g[t][:].indirect(l1[:]), root_z[:, t, :], ALU.mult)
-        for t in range(PACK):
-            nc.scalar.activation(win_abs[t][:, :S], banks[4 + t][:], ACT.Abs)
-            nc.sync.dma_start(own_abs[t][:], win_abs[t][:, :S])
+        def scaled_pick(t):
+            nc.scalar.activation(win_g[t][:, :S], win_y[t][:, :S], ACT.Copy, scale=gn_sb[:, t : t + 1])
+            nc.vector.tensor_copy(picked[:, t, :], win_g[t][:].indirect(l1[:]))
+
+        inverse(0, den_ps[0])
+        scaled_pick(0)
+        scaled_pick(1)
+        inverse(1, den_ps[1])
+        scaled_pick(2)
+        scaled_pick(3)
+        inverse(2, den_ps[2])
+        inverse(3, den_ps[3])
+        nc.scalar.copy(dealt(w3q[0], 0, 128), raw_view(w3_raw))
         nc.scalar.copy(dealt(w2q[0], 0, 128), raw_view(w2_raw))
-        nc.vector.tensor_tensor(woven_out(zq), woven_in(z_planes), woven_in(root_z), ALU.mult)
-        den_b = [den[0][:], den[1][:], den[2][:], den[3][:]]
-        size_sum(den_b[0], 0, l6)
+        inv_ps = banks("inv_ps", "turned")
+        for b in range(S // P):
+            for t in range(PACK):
+                nc.tensor.transpose(inv_ps[b][:, block(t)], inv[t][:, block(b)], ident[:])
+            nc.vector.tensor_tensor(
+                woven_out(zq)[:, 32 * b : 32 * (b + 1)], woven_in(picked[:, :, block(b)]),
+                woven_in(inv_ps[b][:].rearrange("p (t c) -> p t c", t=PACK)), ALU.mult,
+            )
+        quantize(w3q, 0, 512)
+        b_ps = banks("b_ps", "product")
+        for t in range(PACK):
+            product(b_ps[t], w3q, t, z2q[1], z2q[2])
+            nc.scalar.activation(win_abs[t][:, :S], b_ps[t][:], ACT.Abs)
         quantize(zq, 0, 512)
         quantize(w2q, 0, 512)
+        a_ps = banks("a_ps", "product")
+        a_own, diff, res = gated, sig, other
         for t in range(PACK):
-            product(banks[t], w2q, t, zq[1], zq[2])
-        for t in range(1, PACK):
-            size_sum(den_b[t], t, l6)
+            product(a_ps[t], w2q, t, zq[1], zq[2])
+            nc.scalar.activation(win_y[t][:, :S], a_ps[t][:], ACT.Copy)
+            if t == 0:
+                nc.scalar.activation(a_own[t][:], a_ps[t][:], ACT.Copy)
+            else:
+                nc.sync.dma_start(a_own[t][:], win_y[t][:, :S])
 
-        diff, res = root, inv
+        den_b_ps = banks("den_b_ps", "turned")
+        for t in range(PACK):
+            size_sum(den_b_ps[t], t, l6)
+            inverse(t, den_b_ps[t])
+        inv_b_ps = banks("inv_b_ps", "turned")
+        for t in range(PACK):
+            for b in range(S // P):
+                nc.tensor.transpose(inv_b_ps[t][:, block(b)], inv[t][:, block(b)], ident[:])
         out_rows = out.rearrange("(p t) n -> p t n", t=PACK)
-
-        def inverse_b(t):
-            nc.scalar.activation(root_b[t][:], den_b[t], ACT.Abs_reciprocal_sqrt, bias=0.5)
-            nc.scalar.activation(inv_b[t][:], root_b[t][:], ACT.Square)
 
         def difference(t, cols):
             offsets = l5[:, cols.start // 16 : cols.stop // 16]
             nc.vector.tensor_tensor(diff[t][:, cols], win_y[t][:].indirect(offsets), a_own[t][:, cols], ALU.subtract)
 
         def join(t, cols):
-            nc.vector.scalar_tensor_tensor(res[t][:, cols], diff[t][:, cols], -1.0, inv_b[t][:, cols], ALU.mult, ALU.mult)
+            nc.vector.scalar_tensor_tensor(res[t][:, cols], diff[t][:, cols], -1.0, inv_b_ps[t][:, cols], ALU.mult, ALU.mult)
             nc.sync.dma_start(out_rows[:, t, cols], res[t][:, cols])
 
         whole = slice(0, S)
         halves = (slice(0, S // 2), slice(S // 2, S))
-        inverse_b(0)
-        for t in range(PACK):
-            nc.scalar.activation(win_y[t][:, :S], banks[t][:], ACT.Copy)
-            if t < 1:
-                nc.scalar.activation(a_own[t][:], banks[t][:], ACT.Copy)
-            else:
-                nc.sync.dma_start(a_own[t][:], win_y[t][:, :S])
-        for t in range(1, PACK):
-            inverse_b(t)
         difference(0, whole)
         difference(1, whole)
         join(0, whole)
-        join(1, whole)
         difference(2, whole)
+        join(1, whole)
         difference(3, halves[0])
         join(2, whole)
         difference(3, halves[1])

@@ -3,8 +3,9 @@ from contextlib import ExitStack
 import concourse.mybir as mybir
 from concourse.masks import make_identity
 
-K, T, S, N, H = 512, 2048, 512, 512, 512
-FLOPS = 3 * 2 * 512 * 512 * 512
+T = 2048
+S = 512
+FLOPS = 3 * 2 * S * S * S
 
 F32 = mybir.dt.float32
 BF16 = mybir.dt.bfloat16
@@ -18,7 +19,10 @@ ACT = mybir.ActivationFunctionType
 
 P = 128
 PACK = 4
-WIN = 2 * S
+RUN = 4
+PER_COLUMN = 16
+HALF = S // 2
+FIRST, SECOND, WHOLE = slice(0, HALF), slice(HALF, S), slice(0, S)
 
 
 def tile_picked_forknormbnorm2gmax_none_p_kernel(
@@ -30,215 +34,228 @@ def tile_picked_forknormbnorm2gmax_none_p_kernel(
         psum = ctx.enter_context(tc.psum_pool(name="psum", bufs=1))
 
         def f32_tiles(name, width):
-            return [keep.tile([P, width], F32, name="%s%d" % (name, t)) for t in range(PACK)]
+            return [keep.tile([P, width], F32, name="%s%d" % (name, t), align_bytes=64) for t in range(PACK)]
 
-        def load_list(name, src):
-            tile = keep.tile([P, S // 16], U16, name=name)
-            nc.sync.dma_start(tile[:], src)
-            return tile
-
-        warm = keep.tile([P, 1], F32, name="warm")
-        warm_out = keep.tile([P, 1], F32, name="warm_out")
-        xs = keep.tile([P, T], U8, name="xs")
-        nc.gpsimd.memset(xs[:].bitcast(I32), 0)
-        nc.vector.memset(warm[:], 0.0)
-        nc.scalar.activation(warm_out[:], warm[:], ACT.Sigmoid)
-
-        l0 = load_list("l0", offs)
-        w1_raw = [keep.tile([P, PACK, H // 2], F32, name="w1_raw%d" % h) for h in range(2)]
-        w1_rows = w1.rearrange("(p j) c -> p j c", j=PACK)
-        nc.sync.dma_start(w1_raw[0][:], w1_rows[:, :, :256])
-        for q in range(4):
-            nc.sync.dma_start(xs[32 * q : 32 * q + 4, :].bitcast(I32), x_scales[0, 4 * q : 4 * q + 4, :].bitcast(I32))
-        xw = keep.tile([P, T], U32, name="xw")
-        nc.sync.dma_start(xw[:].bitcast(I32), x_words[0].rearrange("p n t -> p (n t)").bitcast(I32))
-        nc.sync.dma_start(w1_raw[1][:], w1_rows[:, :, 256:])
-        l4 = load_list("l4", n4)
-        l3 = load_list("l3", n3)
-        l2 = load_list("l2", n2)
-        gm_sb = keep.tile([P, PACK], F32, name="gm_sb")
-        nc.sync.dma_start(gm_sb[:], gm.rearrange("(p t) o -> p (t o)", t=PACK))
-        w3_raw = keep.tile([P, PACK, N], F32, name="w3_raw")
-        nc.sync.dma_start(w3_raw[:], w3.rearrange("(p j) c -> p j c", j=PACK))
-        gn_sb = keep.tile([P, PACK], F32, name="gn_sb")
-        nc.sync.dma_start(gn_sb[:], gn.rearrange("(p t) o -> p (t o)", t=PACK))
-        l1 = load_list("l1", n1)
-        w2_raw = keep.tile([P, PACK, N], F32, name="w2_raw")
-        nc.sync.dma_start(w2_raw[:], w2.rearrange("(p j) c -> p j c", j=PACK))
-        l6 = load_list("l6", n6)
-        l5 = load_list("l5", n5)
-
-        win_y = f32_tiles("win_y", WIN)
-        win_abs = f32_tiles("win_abs", WIN)
-        win_g = f32_tiles("win_g", WIN)
-        for t in range(PACK):
-            nc.vector.memset(win_y[t][:, S:], 0.0)
-            nc.scalar.activation(win_abs[t][:, S:], warm[:].to_broadcast([P, S]), ACT.Copy)
-            nc.scalar.activation(win_g[t][:, S:], warm[:].to_broadcast([P, S]), ACT.Copy)
-
-        xq_s = keep.tile([P, S], U8, name="xq_s", align_bytes=64)
-        nc.vector.tensor_copy(xq_s[:], xs[:].indirect(l0[:]))
-        xq_w = keep.tile([P, S], U32, name="xq_w", align_bytes=64)
-        nc.vector.tensor_copy(xq_w[:], xw[:].indirect(l0[:]))
-
-        def dealt(wb, m0, m1):
-            return wb[:].rearrange("p (t m j) -> p m j t", t=PACK, j=PACK)[:, m0:m1, :, :]
-
-        def raw_view(raw):
-            return raw[:].rearrange("p j (m t) -> p m j t", t=PACK)
-
-        def mx_tiles(name):
-            wb = keep.tile([P, PACK * 512], BF16, name=name + "_bf", align_bytes=64)
-            codes = keep.tile([P, 512], U32, name=name + "_codes", align_bytes=64)
-            scales = keep.tile([P, 512], U8, name=name + "_scales", align_bytes=64)
-            return wb, codes, scales
-
-        def quantize(tiles, c0, c1):
-            wb, codes, scales = tiles
-            nc.vector.quantize_mx(out=codes[:, c0:c1].bitcast(FP8X4), scales=scales[:, c0:c1], in_=wb[:, PACK * c0 : PACK * c1])
-
-        def product(bank, w_tiles, t, codes, scales):
-            cols = slice(t * P, (t + 1) * P)
-            nc.tensor.matmul_mx(
-                out=bank[:], lhsT=w_tiles[1][:, cols].bitcast(FP8X4), lhsT_scale=w_tiles[2][:, cols],
-                rhs=codes[:].bitcast(FP8X4), rhs_scale=scales[:], start=True, stop=True,
-            )
-
-        w1q, w2q, w3q, zq, z2q = (mx_tiles(n) for n in ("w1", "w2", "w3", "z", "z2"))
-        for h in range(2):
-            nc.vector.tensor_copy(dealt(w1q[0], 64 * h, 64 * (h + 1)), raw_view(w1_raw[h]))
         def banks(name, tag):
             return [psum.tile([P, S], F32, name="%s%d" % (name, t), tag="%s%d" % (tag, t)) for t in range(PACK)]
 
-        ident = keep.tile([P, P], F32, name="ident")
-        make_identity(nc, ident[:])
-        y_ps = banks("y_ps", "product")
-        quantize(w1q, 0, 128)
-        quantize(w1q, 128, 256)
-        quantize(w1q, 256, 512)
-        for t in range(PACK):
-            product(y_ps[t], w1q, t, xq_w, xq_s)
+        def load_list(name, source):
+            tile = keep.tile([P, S // PER_COLUMN], U16, name=name)
+            nc.sync.dma_start(tile[:], source)
+            return tile
 
-        far_abs = f32_tiles("far_abs", S)
-        sig = f32_tiles("sig", S)
-        other = f32_tiles("other", S)
-        gated = f32_tiles("gated", S)
-        root = f32_tiles("root", S)
-        inv = f32_tiles("inv", S)
-        larger = keep.tile([P, PACK, S], F32, name="larger")
-        picked = keep.tile([P, PACK, S], F32, name="picked")
-        z2_planes = keep.tile([P, PACK, S // 2], BF16, name="z2_planes")
+        def load_weight(name, source, cols):
+            tile = keep.tile([P, PACK, cols.stop - cols.start], F32, name=name)
+            nc.sync.dma_start(tile[:], source.rearrange("(p j) c -> p j c", j=PACK)[:, :, cols])
+            return tile
 
-        def woven_out(tiles):
-            return tiles[0][:].rearrange("p (c i t) -> p c t i", i=4, t=PACK)
+        def load_gain(name, source):
+            tile = keep.tile([P, PACK], F32, name=name)
+            nc.sync.dma_start(tile[:], source.rearrange("(p t) o -> p (t o)", t=PACK))
+            return tile
 
-        def woven_in(planes):
-            return planes.rearrange("p t (c i) -> p c t i", i=4)
+        def entries(list_tile, cols):
+            return list_tile[:, cols.start // PER_COLUMN : cols.stop // PER_COLUMN]
 
         def block(b):
             return slice(b * P, (b + 1) * P)
 
-        def turned_sum(bank, first, second):
-            for b in range(S // P):
-                nc.tensor.matmul(bank[:, block(b)], lhsT=first[:, block(b)], rhs=ident[:], is_transpose=True, start=True, stop=False)
-                nc.tensor.matmul(bank[:, block(b)], lhsT=second[:, block(b)], rhs=ident[:], is_transpose=True, start=False, stop=True)
+        x_scale_rows = keep.tile([P, T], U8, name="x_scale_rows")
+        nc.gpsimd.memset(x_scale_rows[:].bitcast(I32), 0)
+        offs_sb = load_list("offs_sb", offs)
+        w1_first = load_weight("w1_first", w1, FIRST)
+        for q in range(4):
+            nc.sync.dma_start(
+                x_scale_rows[32 * q : 32 * q + 4, :].bitcast(I32), x_scales[0, 4 * q : 4 * q + 4, :].bitcast(I32)
+            )
+        w1_second = load_weight("w1_second", w1, SECOND)
+        x_word_rows = keep.tile([P, T], U32, name="x_word_rows")
+        nc.sync.dma_start(x_word_rows[:].bitcast(I32), x_words[0].rearrange("p n r -> p (n r)").bitcast(I32))
+        n4_sb = load_list("n4_sb", n4)
+        n3_sb = load_list("n3_sb", n3)
+        w3_raw = load_weight("w3_raw", w3, WHOLE)
+        gn_sb = load_gain("gn_sb", gn)
+        n2_sb = load_list("n2_sb", n2)
+        n1_sb = load_list("n1_sb", n1)
+        gm_sb = load_gain("gm_sb", gm)
+        w2_raw = load_weight("w2_raw", w2, WHOLE)
+        n6_sb = load_list("n6_sb", n6)
+        n5_sb = load_list("n5_sb", n5)
 
-        def size_sum(bank, t, offsets):
-            nc.vector.tensor_copy(far_abs[t][:], win_abs[t][:].indirect(offsets[:]))
-            turned_sum(bank, win_abs[t], far_abs[t])
+        def woven_tile(name):
+            return keep.tile([P, PACK * S], BF16, name=name, align_bytes=64)
 
-        def inverse(t, bank):
-            nc.scalar.activation(root[t][:], bank[:], ACT.Abs_reciprocal_sqrt, bias=0.5)
-            nc.scalar.activation(inv[t][:], root[t][:], ACT.Square)
+        def quantize(name, woven, codes_tag):
+            codes = keep.tile([P, S], U32, name=name + "_codes", tag=codes_tag, align_bytes=64)
+            scales = keep.tile([P, S], U8, name=name + "_scales", align_bytes=64)
+            nc.vector.quantize_mx(out=codes[:].bitcast(FP8X4), scales=scales[:], in_=woven[:])
+            return codes, scales
 
+        def product(bank, weight, t, codes, scales):
+            weight_codes, weight_scales = weight
+            nc.tensor.matmul_mx(
+                out=bank, lhsT=weight_codes[:, block(t)].bitcast(FP8X4), lhsT_scale=weight_scales[:, block(t)],
+                rhs=codes.bitcast(FP8X4), rhs_scale=scales, start=True, stop=True,
+            )
+
+        def dealt_out(woven, walk):
+            return woven[:].rearrange("p (t m j) -> p " + walk, t=PACK, j=PACK)
+
+        def dealt_in(raw, walk):
+            return raw[:].rearrange("p j (m t) -> p " + walk, t=PACK)
+
+        def deal_on_gpsimd(woven, raw):
+            nc.gpsimd.tensor_scalar(dealt_out(woven, "m t j"), dealt_in(raw, "m t j"), 1.0, 0.0, ALU.mult, ALU.add)
+
+        def woven_out(woven, cols):
+            return woven[:, PACK * cols.start : PACK * cols.stop].rearrange("p (c i t) -> p c t i", i=RUN, t=PACK)
+
+        def woven_in(planes):
+            return planes.rearrange("p t (c i) -> p c t i", i=RUN)
+
+        w1_woven, w2_woven, w3_woven, z_woven, z2_woven = (
+            woven_tile(name) for name in ("w1_woven", "w2_woven", "w3_woven", "z_woven", "z2_woven")
+        )
+
+        nc.vector.tensor_copy(dealt_out(w1_woven, "m j t")[:, : P // 2], dealt_in(w1_first, "m j t"))
+        picked_scales = keep.tile([P, S], U8, name="picked_scales", align_bytes=64)
+        nc.vector.tensor_copy(picked_scales[:], x_scale_rows[:].indirect(offs_sb[:]))
+        nc.vector.tensor_copy(dealt_out(w1_woven, "m j t")[:, P // 2 :], dealt_in(w1_second, "m j t"))
+        w1_mx = quantize("w1", w1_woven, "w1_codes")
+
+        win_plain = f32_tiles("win_plain", 2 * S)
+        win_size = f32_tiles("win_size", 2 * S)
+        win_gained = f32_tiles("win_gained", 2 * S)
+        zero = keep.tile([P, 1], F32, name="zero")
+        nc.vector.memset(zero[:], 0.0)
         for t in range(PACK):
-            nc.scalar.activation(win_y[t][:, :S], y_ps[t][:], ACT.Copy)
-            nc.vector.tensor_copy(other[t][:], win_y[t][:].indirect(l4[:]))
-        for t in range(PACK):
-            nc.scalar.activation(sig[t][:], win_y[t][:].indirect(l3[:]), ACT.Sigmoid)
-            nc.vector.tensor_tensor(gated[t][:], win_y[t][:, :S], sig[t][:], ALU.mult)
-            if t > 0:
-                nc.vector.tensor_tensor(larger[:, t - 1, :], gated[t - 1][:], other[t - 1][:], ALU.max)
-        nc.vector.tensor_tensor(larger[:, PACK - 1, :], gated[PACK - 1][:], other[PACK - 1][:], ALU.max)
-        for t in range(PACK):
-            nc.scalar.activation(win_abs[t][:, :S], y_ps[t][:], ACT.Abs)
-        for t in range(PACK):
-            nc.scalar.activation(z2_planes[:, t, :], larger[:, t, S // 2 :], ACT.Copy, scale=gm_sb[:, t : t + 1])
-        nc.scalar.copy(woven_out(z2q)[:, S // 8 :], woven_in(z2_planes[:]))
-        den_ps = banks("den_ps", "turned")
-        size_sum(den_ps[0], 0, l2)
-        gm_wide = gm_sb[:].unsqueeze(1).unsqueeze(3).to_broadcast([P, S // 8, PACK, 4])
-        nc.vector.tensor_tensor(woven_out(z2q)[:, : S // 8], woven_in(larger[:])[:, : S // 8], gm_wide, ALU.mult)
+            nc.vector.memset(win_plain[t][:, S:], 0.0)
+            nc.scalar.activation(win_size[t][:, S:], zero[:].to_broadcast([P, S]), ACT.Sigmoid)
+            nc.scalar.activation(win_gained[t][:, S:], zero[:].to_broadcast([P, S]), ACT.Sigmoid)
+        identity = keep.tile([P, P], F32, name="identity")
+        make_identity(nc, identity[:])
+
+        picked_words = [keep.tile([P, HALF], U32, name="picked_words%d" % h, align_bytes=64) for h in range(2)]
+        y_banks = banks("y_bank", "product")
+        y0_second = psum.tile([P, S], F32, name="y0_second", tag="turned0")
+        y_halves = [[y_banks[t][:, FIRST], y0_second[:, SECOND] if t == 0 else y_banks[t][:, SECOND]] for t in range(PACK)]
+        for h, cols in enumerate((FIRST, SECOND)):
+            nc.vector.tensor_copy(picked_words[h][:], x_word_rows[:].indirect(entries(offs_sb, cols)))
+            product(y_halves[0][h], w1_mx, 0, picked_words[h][:], picked_scales[:, cols])
         for t in range(1, PACK):
-            size_sum(den_ps[t], t, l2)
-        quantize(z2q, 0, 512)
+            for h, cols in enumerate((FIRST, SECOND)):
+                product(y_halves[t][h], w1_mx, t, picked_words[h][:], picked_scales[:, cols])
 
-        def scaled_pick(t):
-            nc.scalar.activation(win_g[t][:, :S], win_y[t][:, :S], ACT.Copy, scale=gn_sb[:, t : t + 1])
-            nc.vector.tensor_copy(picked[:, t, :], win_g[t][:].indirect(l1[:]))
+        def copy_out_y(window, t, func):
+            if t == 0:
+                for h, cols in enumerate((FIRST, SECOND)):
+                    nc.scalar.activation(window[:, cols], y_halves[t][h], func)
+            else:
+                nc.scalar.activation(window[:, WHOLE], y_banks[t][:], func)
 
-        inverse(0, den_ps[0])
-        scaled_pick(0)
-        scaled_pick(1)
-        inverse(1, den_ps[1])
-        scaled_pick(2)
-        scaled_pick(3)
-        inverse(2, den_ps[2])
-        inverse(3, den_ps[3])
-        nc.scalar.copy(dealt(w3q[0], 0, 128), raw_view(w3_raw))
-        nc.scalar.copy(dealt(w2q[0], 0, 128), raw_view(w2_raw))
-        inv_ps = banks("inv_ps", "turned")
+        def inverse_of_size_sum(bank, root, inverse):
+            nc.scalar.activation(root[:], bank[:], ACT.Abs_reciprocal_sqrt, bias=0.5)
+            nc.scalar.activation(inverse[:], root[:], ACT.Square)
+
+        def size_sum(bank, t, list_tile, far):
+            nc.vector.tensor_copy(far[:], win_size[t][:].indirect(list_tile[:]))
+            for b in range(S // P):
+                for first, term in ((True, win_size[t]), (False, far)):
+                    nc.tensor.matmul(
+                        bank[:, block(b)], lhsT=term[:, block(b)], rhs=identity[:],
+                        is_transpose=True, start=first, stop=not first,
+                    )
+
+        y_at_n4 = f32_tiles("y_at_n4", S)
+        far_size = f32_tiles("far_size", S)
+        y_at_n1 = keep.tile([P, PACK, S], F32, name="y_at_n1")
+        gate = f32_tiles("gate", S)
+        gated = f32_tiles("gated", S)
+        deal_on_gpsimd(w3_woven, w3_raw)
+        for t in range(PACK):
+            copy_out_y(win_plain[t], t, ACT.Copy)
+            nc.vector.tensor_copy(y_at_n4[t][:], win_plain[t][:].indirect(n4_sb[:]))
+        for t in range(PACK):
+            copy_out_y(win_size[t], t, ACT.Abs)
+        y_sums = banks("y_sum", "turned")
+        for t in range(PACK):
+            size_sum(y_sums[t], t, n2_sb, far_size[t])
+        for t in range(PACK):
+            nc.gpsimd.tensor_scalar(
+                win_gained[t][:, WHOLE], win_plain[t][:, WHOLE], gn_sb[:, t : t + 1], 0.0, ALU.mult, ALU.add
+            )
+            nc.vector.tensor_copy(y_at_n1[:, t, :], win_gained[t][:].indirect(n1_sb[:]))
+        for t in range(PACK):
+            nc.scalar.activation(gate[t][:], win_plain[t][:].indirect(n3_sb[:]), ACT.Sigmoid)
+            nc.gpsimd.tensor_tensor(gated[t][:], win_plain[t][:, WHOLE], gate[t][:], ALU.mult)
+        deal_on_gpsimd(w2_woven, w2_raw)
+
+        larger = keep.tile([P, PACK, S], F32, name="larger")
+        for t in range(PACK):
+            nc.vector.tensor_tensor(larger[:, t, :], gated[t][:], y_at_n4[t][:], ALU.max)
+        w3_mx = quantize("w3", w3_woven, "gated%d" % (PACK - 1))
+        root = f32_tiles("root", S)
+        inverse = f32_tiles("inverse", S)
+        for t in range(PACK):
+            inverse_of_size_sum(y_sums[t], root[t], inverse[t])
+
+        z2_planes = keep.tile([P, PACK, S], BF16, name="z2_planes", align_bytes=64)
+        for t in range(PACK):
+            nc.scalar.activation(z2_planes[:, t, :], larger[:, t, :], ACT.Copy, scale=gm_sb[:, t : t + 1])
+        nc.scalar.copy(woven_out(z2_woven, WHOLE), woven_in(z2_planes[:]))
+
+        z_inverses = banks("z_inverse", "turned")
         for b in range(S // P):
             for t in range(PACK):
-                nc.tensor.transpose(inv_ps[b][:, block(t)], inv[t][:, block(b)], ident[:])
+                nc.tensor.transpose(z_inverses[b][:, block(t)], inverse[t][:, block(b)], identity[:])
             nc.vector.tensor_tensor(
-                woven_out(zq)[:, 32 * b : 32 * (b + 1)], woven_in(picked[:, :, block(b)]),
-                woven_in(inv_ps[b][:].rearrange("p (t c) -> p t c", t=PACK)), ALU.mult,
+                woven_out(z_woven, block(b)), woven_in(y_at_n1[:, :, block(b)]),
+                woven_in(z_inverses[b][:].rearrange("p (t c) -> p t c", t=PACK)), ALU.mult,
             )
-        quantize(w3q, 0, 512)
-        b_ps = banks("b_ps", "product")
-        for t in range(PACK):
-            product(b_ps[t], w3q, t, z2q[1], z2q[2])
-            nc.scalar.activation(win_abs[t][:, :S], b_ps[t][:], ACT.Abs)
-        quantize(zq, 0, 512)
-        quantize(w2q, 0, 512)
-        a_ps = banks("a_ps", "product")
-        a_own, diff, res = gated, sig, other
-        for t in range(PACK):
-            product(a_ps[t], w2q, t, zq[1], zq[2])
-            nc.scalar.activation(win_y[t][:, :S], a_ps[t][:], ACT.Copy)
-            if t == 0:
-                nc.scalar.activation(a_own[t][:], a_ps[t][:], ACT.Copy)
-            else:
-                nc.sync.dma_start(a_own[t][:], win_y[t][:, :S])
 
-        den_b_ps = banks("den_b_ps", "turned")
+        z2_codes, z2_scales = quantize("z2", z2_woven, "z2_codes")
+        b_banks = banks("b_bank", "product")
         for t in range(PACK):
-            size_sum(den_b_ps[t], t, l6)
-            inverse(t, den_b_ps[t])
-        inv_b_ps = banks("inv_b_ps", "turned")
+            product(b_banks[t][:], w3_mx, t, z2_codes[:], z2_scales[:])
+            nc.scalar.activation(win_size[t][:, WHOLE], b_banks[t][:], ACT.Abs)
+        z_codes, z_scales = quantize("z", z_woven, "z2_planes")
+        w2_mx = quantize("w2", w2_woven, "z2_woven")
+        a_banks = banks("a_bank", "product")
+        a_again = f32_tiles("a_again", S)
+        for t in range(PACK):
+            product(a_banks[t][:], w2_mx, t, z_codes[:], z_scales[:])
+            nc.scalar.activation(win_plain[t][:, WHOLE], a_banks[t][:], ACT.Copy)
+            if t == 0:
+                nc.scalar.activation(a_again[t][:], a_banks[t][:], ACT.Copy)
+            else:
+                nc.sync.dma_start(a_again[t][:], win_plain[t][:, WHOLE])
+
+        b_sums = banks("b_sum", "turned")
+        for t in range(PACK):
+            size_sum(b_sums[t], t, n6_sb, far_size[t])
+            inverse_of_size_sum(b_sums[t], root[t], inverse[t])
+        out_inverses = banks("out_inverse", "turned")
         for t in range(PACK):
             for b in range(S // P):
-                nc.tensor.transpose(inv_b_ps[t][:, block(b)], inv[t][:, block(b)], ident[:])
+                nc.tensor.transpose(out_inverses[t][:, block(b)], inverse[t][:, block(b)], identity[:])
+        far_less_own = f32_tiles("far_less_own", S)
+        result = f32_tiles("result", S)
         out_rows = out.rearrange("(p t) n -> p t n", t=PACK)
 
-        def difference(t, cols):
-            offsets = l5[:, cols.start // 16 : cols.stop // 16]
-            nc.vector.tensor_tensor(diff[t][:, cols], win_y[t][:].indirect(offsets), a_own[t][:, cols], ALU.subtract)
+        def subtract(t, cols):
+            nc.vector.tensor_tensor(
+                far_less_own[t][:, cols], win_plain[t][:].indirect(entries(n5_sb, cols)), a_again[t][:, cols], ALU.subtract
+            )
 
-        def join(t, cols):
-            nc.vector.scalar_tensor_tensor(res[t][:, cols], diff[t][:, cols], -1.0, inv_b_ps[t][:, cols], ALU.mult, ALU.mult)
-            nc.sync.dma_start(out_rows[:, t, cols], res[t][:, cols])
+        def divide_and_store(t, cols):
+            nc.vector.scalar_tensor_tensor(
+                result[t][:, cols], far_less_own[t][:, cols], -1.0, out_inverses[t][:, cols], ALU.mult, ALU.mult
+            )
+            nc.sync.dma_start(out_rows[:, t, cols], result[t][:, cols])
 
-        whole = slice(0, S)
-        halves = (slice(0, S // 2), slice(S // 2, S))
-        difference(0, whole)
-        difference(1, whole)
-        join(0, whole)
-        difference(2, whole)
-        join(1, whole)
-        difference(3, halves[0])
-        join(2, whole)
-        difference(3, halves[1])
-        for cols in halves:
-            join(3, cols)
+        pieces = [(t, WHOLE) for t in range(PACK - 1)] + [(PACK - 1, FIRST), (PACK - 1, SECOND)]
+        for step in range(len(pieces) + 1):
+            if step < len(pieces):
+                subtract(*pieces[step])
+            if step > 0:
+                divide_and_store(*pieces[step - 1])

from contextlib import ExitStack

import concourse.mybir as mybir
from concourse.masks import make_identity

T = 2048
S = 512
FLOPS = 3 * 2 * S * S * S

F32 = mybir.dt.float32
BF16 = mybir.dt.bfloat16
I32 = mybir.dt.int32
U32 = mybir.dt.uint32
U16 = mybir.dt.uint16
U8 = mybir.dt.uint8
FP8X4 = mybir.dt.float8_e4m3fn_x4
ALU = mybir.AluOpType
ACT = mybir.ActivationFunctionType

P = 128
PACK = 4
RUN = 4
PER_COLUMN = 16
HALF = S // 2
FIRST, SECOND, WHOLE = slice(0, HALF), slice(HALF, S), slice(0, S)


def tile_picked_forknormbnorm2gmax_none_p_kernel(
    tc, x_words, x_scales, w1, gn, w2, gm, w3, offs, n1, n2, n3, n4, n5, n6, out
):
    nc = tc.nc
    with ExitStack() as ctx:
        keep = ctx.enter_context(tc.tile_pool(name="keep", bufs=1))
        psum = ctx.enter_context(tc.psum_pool(name="psum", bufs=1))

        def f32_tiles(name, width):
            return [keep.tile([P, width], F32, name="%s%d" % (name, t), align_bytes=64) for t in range(PACK)]

        def banks(name, tag):
            return [psum.tile([P, S], F32, name="%s%d" % (name, t), tag="%s%d" % (tag, t)) for t in range(PACK)]

        def load_list(name, source):
            tile = keep.tile([P, S // PER_COLUMN], U16, name=name)
            nc.sync.dma_start(tile[:], source)
            return tile

        def load_weight(name, source, cols):
            tile = keep.tile([P, PACK, cols.stop - cols.start], F32, name=name)
            nc.sync.dma_start(tile[:], source.rearrange("(p j) c -> p j c", j=PACK)[:, :, cols])
            return tile

        def load_gain(name, source):
            tile = keep.tile([P, PACK], F32, name=name)
            nc.sync.dma_start(tile[:], source.rearrange("(p t) o -> p (t o)", t=PACK))
            return tile

        def entries(list_tile, cols):
            return list_tile[:, cols.start // PER_COLUMN : cols.stop // PER_COLUMN]

        def block(b):
            return slice(b * P, (b + 1) * P)

        x_scale_rows = keep.tile([P, T], U8, name="x_scale_rows")
        nc.gpsimd.memset(x_scale_rows[:].bitcast(I32), 0)
        offs_sb = load_list("offs_sb", offs)
        w1_first = load_weight("w1_first", w1, FIRST)
        for q in range(4):
            nc.sync.dma_start(
                x_scale_rows[32 * q : 32 * q + 4, :].bitcast(I32), x_scales[0, 4 * q : 4 * q + 4, :].bitcast(I32)
            )
        w1_second = load_weight("w1_second", w1, SECOND)
        x_word_rows = keep.tile([P, T], U32, name="x_word_rows")
        nc.sync.dma_start(x_word_rows[:].bitcast(I32), x_words[0].rearrange("p n r -> p (n r)").bitcast(I32))
        n4_sb = load_list("n4_sb", n4)
        n3_sb = load_list("n3_sb", n3)
        w3_raw = load_weight("w3_raw", w3, WHOLE)
        gn_sb = load_gain("gn_sb", gn)
        n2_sb = load_list("n2_sb", n2)
        n1_sb = load_list("n1_sb", n1)
        gm_sb = load_gain("gm_sb", gm)
        w2_raw = load_weight("w2_raw", w2, WHOLE)
        n6_sb = load_list("n6_sb", n6)
        n5_sb = load_list("n5_sb", n5)

        def woven_tile(name):
            return keep.tile([P, PACK * S], BF16, name=name, align_bytes=64)

        def quantize(name, woven, codes_tag):
            codes = keep.tile([P, S], U32, name=name + "_codes", tag=codes_tag, align_bytes=64)
            scales = keep.tile([P, S], U8, name=name + "_scales", align_bytes=64)
            nc.vector.quantize_mx(out=codes[:].bitcast(FP8X4), scales=scales[:], in_=woven[:])
            return codes, scales

        def product(bank, weight, t, codes, scales):
            weight_codes, weight_scales = weight
            nc.tensor.matmul_mx(
                out=bank, lhsT=weight_codes[:, block(t)].bitcast(FP8X4), lhsT_scale=weight_scales[:, block(t)],
                rhs=codes.bitcast(FP8X4), rhs_scale=scales, start=True, stop=True,
            )

        def dealt_out(woven, walk):
            return woven[:].rearrange("p (t m j) -> p " + walk, t=PACK, j=PACK)

        def dealt_in(raw, walk):
            return raw[:].rearrange("p j (m t) -> p " + walk, t=PACK)

        def deal_on_gpsimd(woven, raw):
            nc.gpsimd.tensor_scalar(dealt_out(woven, "m t j"), dealt_in(raw, "m t j"), 1.0, 0.0, ALU.mult, ALU.add)

        def woven_out(woven, cols):
            return woven[:, PACK * cols.start : PACK * cols.stop].rearrange("p (c i t) -> p c t i", i=RUN, t=PACK)

        def woven_in(planes):
            return planes.rearrange("p t (c i) -> p c t i", i=RUN)

        w1_woven, w2_woven, w3_woven, z_woven, z2_woven = (
            woven_tile(name) for name in ("w1_woven", "w2_woven", "w3_woven", "z_woven", "z2_woven")
        )

        nc.vector.tensor_copy(dealt_out(w1_woven, "m j t")[:, : P // 2], dealt_in(w1_first, "m j t"))
        picked_scales = keep.tile([P, S], U8, name="picked_scales", align_bytes=64)
        nc.vector.tensor_copy(picked_scales[:], x_scale_rows[:].indirect(offs_sb[:]))
        nc.vector.tensor_copy(dealt_out(w1_woven, "m j t")[:, P // 2 :], dealt_in(w1_second, "m j t"))
        w1_mx = quantize("w1", w1_woven, "w1_codes")

        win_plain = f32_tiles("win_plain", 2 * S)
        win_size = f32_tiles("win_size", 2 * S)
        win_gained = f32_tiles("win_gained", 2 * S)
        zero = keep.tile([P, 1], F32, name="zero")
        nc.vector.memset(zero[:], 0.0)
        for t in range(PACK):
            nc.vector.memset(win_plain[t][:, S:], 0.0)
            nc.scalar.activation(win_size[t][:, S:], zero[:].to_broadcast([P, S]), ACT.Sigmoid)
            nc.scalar.activation(win_gained[t][:, S:], zero[:].to_broadcast([P, S]), ACT.Sigmoid)
        identity = keep.tile([P, P], F32, name="identity")
        make_identity(nc, identity[:])

        picked_words = [keep.tile([P, HALF], U32, name="picked_words%d" % h, align_bytes=64) for h in range(2)]
        y_banks = banks("y_bank", "product")
        y0_second = psum.tile([P, S], F32, name="y0_second", tag="turned0")
        y_halves = [[y_banks[t][:, FIRST], y0_second[:, SECOND] if t == 0 else y_banks[t][:, SECOND]] for t in range(PACK)]
        for h, cols in enumerate((FIRST, SECOND)):
            nc.vector.tensor_copy(picked_words[h][:], x_word_rows[:].indirect(entries(offs_sb, cols)))
            product(y_halves[0][h], w1_mx, 0, picked_words[h][:], picked_scales[:, cols])
        for t in range(1, PACK):
            for h, cols in enumerate((FIRST, SECOND)):
                product(y_halves[t][h], w1_mx, t, picked_words[h][:], picked_scales[:, cols])

        def copy_out_y(window, t, func):
            if t == 0:
                for h, cols in enumerate((FIRST, SECOND)):
                    nc.scalar.activation(window[:, cols], y_halves[t][h], func)
            else:
                nc.scalar.activation(window[:, WHOLE], y_banks[t][:], func)

        def inverse_of_size_sum(bank, root, inverse):
            nc.scalar.activation(root[:], bank[:], ACT.Abs_reciprocal_sqrt, bias=0.5)
            nc.scalar.activation(inverse[:], root[:], ACT.Square)

        def size_sum(bank, t, list_tile, far):
            nc.vector.tensor_copy(far[:], win_size[t][:].indirect(list_tile[:]))
            for b in range(S // P):
                for first, term in ((True, win_size[t]), (False, far)):
                    nc.tensor.matmul(
                        bank[:, block(b)], lhsT=term[:, block(b)], rhs=identity[:],
                        is_transpose=True, start=first, stop=not first,
                    )

        y_at_n4 = f32_tiles("y_at_n4", S)
        far_size = f32_tiles("far_size", S)
        y_at_n1 = keep.tile([P, PACK, S], F32, name="y_at_n1")
        gate = f32_tiles("gate", S)
        gated = f32_tiles("gated", S)
        deal_on_gpsimd(w3_woven, w3_raw)
        for t in range(PACK):
            copy_out_y(win_plain[t], t, ACT.Copy)
            nc.vector.tensor_copy(y_at_n4[t][:], win_plain[t][:].indirect(n4_sb[:]))
        for t in range(PACK):
            copy_out_y(win_size[t], t, ACT.Abs)
        y_sums = banks("y_sum", "turned")
        for t in range(PACK):
            size_sum(y_sums[t], t, n2_sb, far_size[t])
        for t in range(PACK):
            nc.gpsimd.tensor_scalar(
                win_gained[t][:, WHOLE], win_plain[t][:, WHOLE], gn_sb[:, t : t + 1], 0.0, ALU.mult, ALU.add
            )
            nc.vector.tensor_copy(y_at_n1[:, t, :], win_gained[t][:].indirect(n1_sb[:]))
        for t in range(PACK):
            nc.scalar.activation(gate[t][:], win_plain[t][:].indirect(n3_sb[:]), ACT.Sigmoid)
            nc.gpsimd.tensor_tensor(gated[t][:], win_plain[t][:, WHOLE], gate[t][:], ALU.mult)
        deal_on_gpsimd(w2_woven, w2_raw)

        larger = keep.tile([P, PACK, S], F32, name="larger")
        for t in range(PACK):
            nc.vector.tensor_tensor(larger[:, t, :], gated[t][:], y_at_n4[t][:], ALU.max)
        w3_mx = quantize("w3", w3_woven, "gated%d" % (PACK - 1))
        root = f32_tiles("root", S)
        inverse = f32_tiles("inverse", S)
        for t in range(PACK):
            inverse_of_size_sum(y_sums[t], root[t], inverse[t])

        z2_planes = keep.tile([P, PACK, S], BF16, name="z2_planes", align_bytes=64)
        for t in range(PACK):
            nc.scalar.activation(z2_planes[:, t, :], larger[:, t, :], ACT.Copy, scale=gm_sb[:, t : t + 1])
        nc.scalar.copy(woven_out(z2_woven, WHOLE), woven_in(z2_planes[:]))

        z_inverses = banks("z_inverse", "turned")
        for b in range(S // P):
            for t in range(PACK):
                nc.tensor.transpose(z_inverses[b][:, block(t)], inverse[t][:, block(b)], identity[:])
            nc.vector.tensor_tensor(
                woven_out(z_woven, block(b)), woven_in(y_at_n1[:, :, block(b)]),
                woven_in(z_inverses[b][:].rearrange("p (t c) -> p t c", t=PACK)), ALU.mult,
            )

        z2_codes, z2_scales = quantize("z2", z2_woven, "z2_codes")
        b_banks = banks("b_bank", "product")
        for t in range(PACK):
            product(b_banks[t][:], w3_mx, t, z2_codes[:], z2_scales[:])
            nc.scalar.activation(win_size[t][:, WHOLE], b_banks[t][:], ACT.Abs)
        z_codes, z_scales = quantize("z", z_woven, "z2_planes")
        w2_mx = quantize("w2", w2_woven, "z2_woven")
        a_banks = banks("a_bank", "product")
        a_again = f32_tiles("a_again", S)
        for t in range(PACK):
            product(a_banks[t][:], w2_mx, t, z_codes[:], z_scales[:])
            nc.scalar.activation(win_plain[t][:, WHOLE], a_banks[t][:], ACT.Copy)
            if t == 0:
                nc.scalar.activation(a_again[t][:], a_banks[t][:], ACT.Copy)
            else:
                nc.sync.dma_start(a_again[t][:], win_plain[t][:, WHOLE])

        b_sums = banks("b_sum", "turned")
        for t in range(PACK):
            size_sum(b_sums[t], t, n6_sb, far_size[t])
            inverse_of_size_sum(b_sums[t], root[t], inverse[t])
        out_inverses = banks("out_inverse", "turned")
        for t in range(PACK):
            for b in range(S // P):
                nc.tensor.transpose(out_inverses[t][:, block(b)], inverse[t][:, block(b)], identity[:])
        far_less_own = f32_tiles("far_less_own", S)
        result = f32_tiles("result", S)
        out_rows = out.rearrange("(p t) n -> p t n", t=PACK)

        def subtract(t, cols):
            nc.vector.tensor_tensor(
                far_less_own[t][:, cols], win_plain[t][:].indirect(entries(n5_sb, cols)), a_again[t][:, cols], ALU.subtract
            )

        def divide_and_store(t, cols):
            nc.vector.scalar_tensor_tensor(
                result[t][:, cols], far_less_own[t][:, cols], -1.0, out_inverses[t][:, cols], ALU.mult, ALU.mult
            )
            nc.sync.dma_start(out_rows[:, t, cols], result[t][:, cols])

        pieces = [(t, WHOLE) for t in range(PACK - 1)] + [(PACK - 1, FIRST), (PACK - 1, SECOND)]
        for step in range(len(pieces) + 1):
            if step < len(pieces):
                subtract(*pieces[step])
            if step > 0:
                divide_and_store(*pieces[step - 1])
